import numpy as np
import ml_dtypes


def mxq(x, axis, fmt="e4m3"):
    dtype, down = {"e4m3": (ml_dtypes.float8_e4m3fn, 7), "e5m2": (ml_dtypes.float8_e5m2, 14)}[fmt]
    v = np.moveaxis(np.asarray(x, np.float32).astype(ml_dtypes.bfloat16).astype(np.float64), axis, -1)
    blocks = v.reshape(v.shape[:-1] + (-1, 32))
    amax = np.abs(blocks).max(-1, keepdims=True)
    byte = np.maximum(np.where(amax > 0, np.frexp(amax)[1] - 1 + 127, 0) - down, 1)
    scale = np.exp2(byte - 127.0)
    codes = (blocks / scale).astype(np.float32).astype(dtype).astype(np.float64)
    return np.moveaxis((codes * scale).reshape(v.shape), -1, axis)


WIDE = False


def mx_kscale(k):
    if not WIDE:
        return np.ones(k)
    levels = np.array([10, -10, 5, -5, 0])
    if k % 512:
        return np.exp2(np.random.permutation(np.resize(levels, k // 32))).repeat(32)
    a = np.empty((k // 512, 16))
    for p in range(k // 512):
        a[p, :8] = np.random.permutation(np.resize(levels, 8))
        for g in range(8):
            far = levels[np.abs(levels - a[p, g]) >= 10]
            a[p, g + 8] = far[np.random.randint(len(far))]
    return np.exp2(a.ravel()).repeat(32)


def f64(x):
    return np.asarray(x).astype(np.float64)


def striped(idx):
    return np.tile(idx.reshape(-1, 16).T, (8, 1)).astype(np.uint16)


def unstriped(offs):
    return offs[:16].T.reshape(-1).astype(np.int64)


E2M1 = np.array([0.0, 0.5, 1.0, 1.5, 2.0, 3.0, 4.0, 6.0, -0.0, -0.5, -1.0, -1.5, -2.0, -3.0, -4.0, -6.0])


def pack_weight(w, fmt):
    k, n = w.shape
    w = f64(np.asarray(w, np.float32).astype(ml_dtypes.bfloat16)).reshape(k // 32, 32, n)
    amax = np.abs(w).max(1)
    if fmt == "e4m3":
        byte = np.frexp(amax)[1] - 1 + 127 - 7
    else:
        mant, ex = np.frexp(amax / 6.0)
        byte = np.where(mant > 0.5, ex, ex - 1) + 127
    byte = np.clip(np.where(amax > 0, byte, 1), 1, 254)
    scaled = (w * np.exp2(127.0 - byte)[:, None, :]).reshape(k, n).astype(np.float32)
    by_word = np.ascontiguousarray(scaled.reshape(k // 512, 128, 4, n).transpose(0, 1, 3, 2))
    if fmt == "e4m3":
        words = by_word.astype(ml_dtypes.float8_e4m3fn).view(np.uint8)
    else:
        c = by_word.astype(ml_dtypes.float4_e2m1fn).view(np.uint8) & 0xF
        words = (c[..., 0::2] | (c[..., 1::2] << 4)).reshape(k // 512, 128, 2 * n)
    return np.ascontiguousarray(words), np.ascontiguousarray(byte.astype(np.uint8).reshape(k // 512, 16, n))


def unpack_weight(words, scales, fmt):
    g, _, n = scales.shape
    words = np.ascontiguousarray(words).reshape(g, 128, n, -1)
    if fmt == "e4m3":
        vals = words.view(ml_dtypes.float8_e4m3fn).astype(np.float64)
    else:
        nib = np.empty((g, 128, n, 4), np.uint8)
        nib[..., 0::2] = words & 0xF
        nib[..., 1::2] = words >> 4
        vals = E2M1[nib]
    vals = vals * np.repeat(np.exp2(scales.astype(np.float64) - 127.0), 8, axis=1)[..., None]
    return vals.transpose(0, 1, 3, 2).reshape(g * 512, n)


def gelu(v):
    return 0.5 * v * (1.0 + np.tanh(np.sqrt(2.0 / np.pi) * (v + 0.044715 * v**3)))


def often(T, S):
    return np.random.permutation(T)[(T * np.random.uniform(0, 1, S) ** 4).astype(np.int64)]


def bf(x):
    return np.asarray(x, np.float32).astype(ml_dtypes.bfloat16)


def planes(Y):
    n, m = Y.shape
    b = f64(bf(Y)).reshape(n // 32, 32, m)
    amax = np.abs(b).max(1)
    byte = np.clip(np.where(amax > 0, np.frexp(amax)[1] - 1 + 127 - 7, 1), 1, 254)
    codes = (b * np.exp2(127.0 - byte)[:, None, :]).reshape(n, m).astype(np.float32).astype(ml_dtypes.float8_e4m3fn).view(np.uint8)
    words = codes.reshape(n // 512, 128, 4, m).transpose(0, 1, 3, 2)
    return np.ascontiguousarray(words), np.ascontiguousarray(byte.astype(np.uint8).reshape(n // 512, 16, m))


K, K2, T, S, P, H, N = 512, 1024, 2048, 1024, 512, 1024, 512

def setup_inputs():
    n = np.random.standard_normal
    s, s2, u = mx_kscale(K)[:, None], mx_kscale(K2)[:, None], mx_kscale(H)[:, None]
    d = {}
    d["tab_words"], d["tab_scales"] = pack_weight(n((K, T)) * s, "e4m3")
    d["tab2_words"], d["tab2_scales"] = pack_weight(n((K2, T)) * s2, "e4m3")
    d["tab3_words"], d["tab3_scales"] = pack_weight(n((K, T)) * s, "e4m3")
    d["offs"] = striped(np.random.permutation(T)[:S])
    d["offs2"] = striped(np.random.permutation(T)[:S])
    d["offs3"] = striped(np.random.permutation(T)[:S])
    d["pos1"] = striped(np.random.permutation(S)[:P])
    d["pos2"] = striped(often(S, P))
    d["pos3"] = striped(often(S, P))
    d["wa"] = (n((K, H)) / K**0.5 / s).astype(np.float32)
    d["w4_words"], d["w4_scales"] = pack_weight(n((K2, H)) / K2**0.5 / s2, "e2m1")
    d["w8_words"], d["w8_scales"] = pack_weight(n((K, H)) / K**0.5 / s, "e4m3")
    d["gz"] = (np.exp(0.3 * n(H)) * u[:, 0]).astype(np.float32)
    d["wy"] = (0.5 * n((H, N)) / H**0.5 / u * np.exp(0.8 * n(N))).astype(np.float32)
    return d

def reference(tab_words, tab_scales, tab2_words, tab2_scales, tab3_words, tab3_scales, offs, offs2, offs3,
              pos1, pos2, pos3, wa, w4_words, w4_scales, w8_words, w8_scales, gz, wy):
    v = unpack_weight(tab_words, tab_scales, "e4m3")[:, unstriped(offs)]
    v2 = unpack_weight(tab2_words, tab2_scales, "e4m3")[:, unstriped(offs2)]
    v3 = unpack_weight(tab3_words, tab3_scales, "e4m3")[:, unstriped(offs3)]
    a = mxq(f64(wa), 0, "e4m3").T @ v
    b = unpack_weight(w4_words, w4_scales, "e2m1").T @ v2
    d = unpack_weight(w8_words, w8_scales, "e4m3").T @ v3
    a1 = a[:, unstriped(pos1)]
    b1 = b[:, unstriped(pos2)]
    d1 = d[:, unstriped(pos3)]
    z = f64(gz)[:, None] * (a1 * b1 - np.abs(a1 - b1) + d1)
    y = mxq(f64(wy), 0, "e4m3").T @ mxq(z, 0, "e4m3")
    words, scales = planes(y)
    return y, words, scales

@@ -1,0 +1,288 @@
+from contextlib import ExitStack
+
+import concourse.mybir as mybir
+from concourse.masks import make_identity
+
+K, K2, T, S, NU, H, N = 512, 1024, 2048, 1024, 512, 1024, 512
+FLOPS = 2 * (K + K2 + K) * H * S + 2 * H * N * NU
+
+F32 = mybir.dt.float32
+BF16 = mybir.dt.bfloat16
+I32 = mybir.dt.int32
+U32 = mybir.dt.uint32
+U16 = mybir.dt.uint16
+U8 = mybir.dt.uint8
+FP8X4 = mybir.dt.float8_e4m3fn_x4
+FP4X4 = mybir.dt.float4_e2m1fn_x4
+MULT = mybir.AluOpType.mult
+ADD = mybir.AluOpType.add
+COPY = mybir.ActivationFunctionType.Copy
+ABS = mybir.ActivationFunctionType.Abs
+
+P = 128
+BANK = 512
+QUADS = 4
+
+
+def tile_list_graft_union_features_kernel(
+    tc, tab_words, tab_scales, tab2_words, tab2_scales, tab3_words, tab3_scales, offs, offs2, offs3,
+    pos1, pos2, pos3, wa, w4_words, w4_scales, w8_words, w8_scales, gz, wy, out_0, out_1, out_2,
+):
+    nc = tc.nc
+    with ExitStack() as ctx:
+        lists = ctx.enter_context(tc.tile_pool(name="lists", bufs=1))
+        keep = ctx.enter_context(tc.tile_pool(name="keep", bufs=1))
+        ring = ctx.enter_context(tc.tile_pool(name="ring", bufs=2))
+        psum = ctx.enter_context(tc.psum_pool(name="psum", bufs=2))
+
+        def load_list(src, name):
+            tile = lists.tile(list(src.shape), U16, name=name)
+            nc.sync.dma_start(tile[:], src)
+            return tile
+
+        def zeroed_plane(shape, name):
+            tile = keep.tile(shape, U8, name=name, align_bytes=64)
+            nc.vector.memset(tile[:].bitcast(I32), 0)
+            return tile
+
+        def load_table_scales(src, name):
+            passes = src.shape[0]
+            tile = zeroed_plane([P, T], name)
+            for q in range(QUADS):
+                nc.scalar.dma_start(
+                    tile[32 * q : 32 * q + 4 * passes, :].bitcast(I32), src[:, 4 * q : 4 * q + 4, :].bitcast(I32)
+                )
+            return tile
+
+        def load_weight_scales(src, name, queue):
+            passes = src.shape[0]
+            tile = zeroed_plane([P, passes, H], name)
+            for q in range(QUADS):
+                queue.dma_start(
+                    tile[32 * q : 32 * q + 4, :, :].bitcast(I32),
+                    src[:, 4 * q : 4 * q + 4, :].rearrange("a r n -> r a n").bitcast(I32),
+                )
+            return tile
+
+        def load_table_words(src, tag):
+            tile = keep.tile([P, T], U32, name=tag, tag=tag, align_bytes=64)
+            nc.sync.dma_start(tile[:].bitcast(I32), src.rearrange("p t i -> p (t i)").bitcast(I32))
+            return tile
+
+        def gather_bytes(window, offsets, dtype, name):
+            tile = keep.tile([P, S], dtype, name=name, align_bytes=64)
+            nc.vector.tensor_copy(tile[:], window[:].indirect(offsets[:]))
+            return tile
+
+        ident = keep.tile([P, P], F32, name="ident")
+        make_identity(nc, ident[:])
+
+        idx3 = load_list(offs3, "idx3")
+        t3s = load_table_scales(tab3_scales, "t3s")
+        t3w = load_table_words(tab3_words[0], "big0")
+        idx1 = load_list(offs, "idx1")
+        t1w = load_table_words(tab_words[0], "big1")
+        w8s = load_weight_scales(w8_scales, "w8s", nc.scalar)
+        w8w = keep.tile([P, H], U32, name="w8w", align_bytes=64)
+        nc.sync.dma_start(w8w[:].bitcast(I32), w8_words[0].rearrange("p c i -> p (c i)").bitcast(I32))
+        t1s = load_table_scales(tab_scales, "t1s")
+        idx2 = load_list(offs2, "idx2")
+        wa_raw = []
+        for h in range(2):
+            raw = ring.tile([P, 4, BANK], F32, name="raw", tag="raw", align_bytes=64)
+            nc.sync.dma_start(raw[:], wa[:, h * BANK : (h + 1) * BANK].rearrange("(p t) c -> p t c", t=4))
+            wa_raw.append(raw)
+        t2s = load_table_scales(tab2_scales, "t2s")
+        t2w = [load_table_words(tab2_words[a], "big%d" % (2 + a)) for a in range(2)]
+        p3 = load_list(pos3, "p3")
+        w4w = keep.tile([P, 2, 2 * H], U8, name="w4w", align_bytes=64)
+        nc.sync.dma_start(w4w[:].bitcast(I32), w4_words.rearrange("a p b -> p a b").bitcast(I32))
+        w4s = load_weight_scales(w4_scales, "w4s", nc.sync)
+        p1 = load_list(pos1, "p1")
+        p2 = load_list(pos2, "p2")
+        gain = keep.tile([P, H], F32, name="gain")
+        nc.sync.dma_start(gain[:], gz.partition_broadcast(P))
+
+        def first_stage(s, passes, tag, bufs, sign):
+            window = ring.tile([P, S], F32, name=tag, tag=tag, bufs=bufs)
+            for h in range(S // BANK):
+                cols = slice(h * BANK, (h + 1) * BANK)
+                acc = psum.tile([P, BANK], F32, name="mm", tag="mm", bufs=4)
+                for i, (w, ws, v, vs) in enumerate(passes):
+                    nc.tensor.matmul_mx(
+                        out=acc[:], lhsT=w, lhsT_scale=ws, rhs=v[:, cols].bitcast(FP8X4), rhs_scale=vs[:, cols],
+                        start=(i == 0), stop=(i == len(passes) - 1),
+                    )
+                nc.scalar.activation(window[:, cols], acc[:], COPY, scale=sign)
+            return window
+
+        def quantise(grouped, codes, scales):
+            nc.vector.quantize_mx(out=codes.bitcast(FP8X4), scales=scales, in_=grouped)
+
+        v3s = gather_bytes(t3s, idx3, U8, "v3s")
+        v3w = gather_bytes(t3w, idx3, U32, "v3w")
+        rows = [slice(s * P, (s + 1) * P) for s in range(H // P)]
+        d_win = [
+            first_stage(s, [(w8w[:, rows[s]].bitcast(FP8X4), w8s[:, 0, rows[s]], v3w, v3s)], "d_win", 8, -1.0)
+            for s in range(H // P)
+        ]
+        v1w = gather_bytes(t1w, idx1, U32, "v1w")
+        v1s = gather_bytes(t1s, idx1, U8, "v1s")
+        v2s = gather_bytes(t2s, idx2, U8, "v2s")
+        v2s_hi = zeroed_plane([P, S], "v2s_hi")
+        nc.sync.dma_start(v2s_hi[0 : P - 4, :].bitcast(I32), v2s[4:P, :].bitcast(I32))
+        wa_c, wa_s = [], []
+        for h in range(2):
+            grouped = ring.tile([P, 4 * BANK], BF16, name="grouped", tag="grouped", bufs=3, align_bytes=64)
+            nc.gpsimd.tensor_scalar(
+                grouped[:].rearrange("p (c t) -> p c t", t=4), wa_raw[h][:].rearrange("p t c -> p c t"),
+                1.0, 0.0, MULT, ADD,
+            )
+            codes = keep.tile([P, BANK], U32, name="wa_c%d" % h, align_bytes=64)
+            scales = keep.tile([P, BANK], U8, name="wa_s%d" % h, align_bytes=64)
+            quantise(grouped[:], codes[:], scales[:])
+            wa_c.append(codes)
+            wa_s.append(scales)
+        v2w = [gather_bytes(t2w[a], idx2, U32, "v2w%d" % a) for a in range(2)]
+        v2_planes = [v2s, v2s_hi]
+
+        def pick(window, positions, lo, hi, tag, bufs):
+            tile = ring.tile([P, hi - lo], F32, name=tag, tag=tag, bufs=bufs)
+            nc.vector.tensor_copy(tile[:], window[:].indirect(positions[:, lo // 16 : hi // 16]))
+            return tile
+
+        a_win, b_win = {}, {}
+
+        def scions_and_rootstocks(s):
+            local = slice((s % 4) * P, (s % 4 + 1) * P)
+            a_win[s] = first_stage(
+                s, [(wa_c[s // 4][:, local].bitcast(FP8X4), wa_s[s // 4][:, local], v1w, v1s)], "a_win", 5, 1.0
+            )
+            b_win[s] = first_stage(
+                s,
+                [
+                    (w4w[:, a, 2 * s * P : 2 * (s + 1) * P].bitcast(FP4X4), w4s[:, a, rows[s]], v2w[a], v2_planes[a])
+                    for a in range(2)
+                ],
+                "b_win", 5, -1.0,
+            )
+
+        def join(s, lo, hi, d1, z_t):
+            width = hi - lo
+            blocks = width // P
+            a1 = pick(a_win[s], p1, lo, hi, "a1", 3)
+            b1 = pick(b_win[s], p2, lo, hi, "b1", 3)
+            diff = ring.tile([P, width], F32, name="diff", tag="diff", bufs=2)
+            nc.gpsimd.tensor_tensor(diff[:], a1[:], b1[:], ADD)
+            prod = ring.tile([P, width], F32, name="prod", tag="prod", bufs=2)
+            nc.gpsimd.tensor_tensor(prod[:], a1[:], b1[:], MULT)
+            dist = ring.tile([P, width], F32, name="dist", tag="dist", bufs=2)
+            nc.scalar.activation(dist[:], diff[:], ABS)
+            total = psum.tile([P, blocks, P], F32, name="total", tag="total")
+            terms = (d1, prod, dist)
+            for i, term in enumerate(terms):
+                for b in range(blocks):
+                    nc.tensor.matmul(
+                        total[:, b, :], term[:, b * P : (b + 1) * P], ident[:], is_transpose=True,
+                        start=(i == 0 and b == 0), stop=(i == len(terms) - 1 and b == blocks - 1),
+                    )
+            nc.vector.scalar_tensor_tensor(
+                z_t[:, :, (s % 4) * P : (s % 4 + 1) * P], total[:], -1.0,
+                gain[:, rows[s]].unsqueeze(1).to_broadcast([P, blocks, P]), MULT, MULT,
+            )
+
+        z_c, z_s = {}, {}
+
+        def turn_and_quantise(g, half, z_t, first_block):
+            words = z_t[:].rearrange("p b r -> p (b r)").bitcast(F32)
+            turned = psum.tile([P, 2, 2, P], F32, name="turned", tag="turned")
+            for b in range(2):
+                base = (first_block + b) * 256
+                for u in range(2):
+                    nc.tensor.transpose(turned[:, b, u, :], words[:, base + u : base + 256 : 2], ident[:])
+            grouped = ring.tile([P, 4 * 256], BF16, name="grouped", tag="grouped", bufs=3, align_bytes=64)
+            nc.scalar.copy(
+                grouped[:].bitcast(F32).rearrange("p (b j u) -> p b j u", b=2, u=2),
+                turned[:].rearrange("p b u j -> p b j u"),
+            )
+            z_c[g, half] = keep.tile([P, 256], U32, name="z_c%d%d" % (g, half), align_bytes=64)
+            z_s[g, half] = keep.tile([P, 256], U8, name="z_s%d%d" % (g, half), align_bytes=64)
+            quantise(grouped[:], z_c[g, half][:], z_s[g, half][:])
+
+        d1_first = [pick(d_win[s], p3, 0, NU, "d1", 4) for s in range(4)]
+        d1_a = [pick(d_win[s], p3, 0, 256, "d1h", 4) for s in range(4, 8)]
+
+        scions_and_rootstocks(0)
+        scions_and_rootstocks(1)
+        z_t0 = keep.tile([P, 4, BANK], BF16, name="z_t0", tag="big2", align_bytes=64)
+        for s in range(4):
+            scions_and_rootstocks(s + 2)
+            join(s, 0, NU, d1_first[s], z_t0)
+
+        wy_c, wy_s = [], []
+        for g in range(2):
+            raw = keep.tile([P, 4, N], F32, name="wy_raw", tag="big%d" % g, align_bytes=64)
+            nc.sync.dma_start(raw[:], wy[g * 512 : (g + 1) * 512, :].rearrange("(p j) n -> p j n", j=4))
+            grouped = ring.tile([P, 4 * N], BF16, name="grouped", tag="grouped", bufs=3, align_bytes=64)
+            nc.scalar.copy(
+                grouped[:].rearrange("p (t m j) -> p m j t", t=4, j=4),
+                raw[:].rearrange("p j (m t) -> p m j t", t=4),
+            )
+            codes = keep.tile([P, N], U32, name="wy_c%d" % g, align_bytes=64)
+            scales = keep.tile([P, N], U8, name="wy_s%d" % g, align_bytes=64)
+            quantise(grouped[:], codes[:], scales[:])
+            wy_c.append(codes)
+            wy_s.append(scales)
+
+        scions_and_rootstocks(6)
+        scions_and_rootstocks(7)
+        for half in range(2):
+            turn_and_quantise(0, half, z_t0, 2 * half)
+
+        y_acc = [psum.tile([P, 4, P], F32, name="mm", tag="mm", bufs=4) for b in range(4)]
+
+        def last_stage(g, block):
+            cols = slice((block % 2) * P, (block % 2 + 1) * P)
+            for t in range(4):
+                nc.tensor.matmul_mx(
+                    out=y_acc[block][:, t, :],
+                    lhsT=wy_c[g][:, t * P : (t + 1) * P].bitcast(FP8X4), lhsT_scale=wy_s[g][:, t * P : (t + 1) * P],
+                    rhs=z_c[g, block // 2][:, cols].bitcast(FP8X4), rhs_scale=z_s[g, block // 2][:, cols],
+                    start=(g == 0 and t == 0), stop=(g == 1 and t == 3),
+                )
+
+        y_codes = keep.tile([P, NU], U32, name="y_codes", align_bytes=64)
+        y_scales = keep.tile([P, NU], U8, name="y_scales", align_bytes=64)
+        y_rows = out_0.rearrange("(p t) j -> p t j", t=4)
+        code_rows = out_1[0].rearrange("p m t -> p (m t)").bitcast(I32)
+
+        z_t1 = ring.tile([P, 2, BANK], BF16, name="z_t1", tag="z_t1", align_bytes=64)
+        for s in range(4, 8):
+            join(s, 0, 256, d1_a[s - 4], z_t1)
+        for block in range(4):
+            last_stage(0, block)
+        for half in range(2):
+            if half == 1:
+                z_t1 = ring.tile([P, 2, BANK], BF16, name="z_t1", tag="z_t1", align_bytes=64)
+                for s in range(4, 8):
+                    join(s, 256, NU, pick(d_win[s], p3, 256, NU, "d1h", 4), z_t1)
+            turn_and_quantise(1, half, z_t1, 0)
+            y_sb = ring.tile([P, 4, 256], F32, name="raw", tag="raw", align_bytes=64)
+            for b in range(2):
+                block = 2 * half + b
+                last_stage(1, block)
+                grouped = ring.tile([P, 4 * P], BF16, name="grouped", tag="grouped", bufs=3, align_bytes=64)
+                nc.vector.tensor_copy(
+                    grouped[:].rearrange("p (j t) -> p j t", t=4), y_acc[block][:].rearrange("p t j -> p j t")
+                )
+                nc.scalar.copy(y_sb[:, :, b * P : (b + 1) * P], y_acc[block][:])
+                cols = slice(block * P, (block + 1) * P)
+                quantise(grouped[:], y_codes[:, cols], y_scales[:, cols])
+            cols = slice(half * 256, (half + 1) * 256)
+            nc.sync.dma_start(y_rows[:, :, cols], y_sb[:])
+            nc.sync.dma_start(code_rows[:, cols], y_codes[:, cols].bitcast(I32))
+        for q in range(QUADS):
+            queue = nc.sync if q % 2 == 0 else nc.scalar
+            queue.dma_start(
+                out_2[0, 4 * q : 4 * q + 4, :].bitcast(I32), y_scales[32 * q : 32 * q + 4, :].bitcast(I32)
+            )

@@ -15,7 +15,9 @@ U8 = mybir.dt.uint8
 FP8X4 = mybir.dt.float8_e4m3fn_x4
 FP4X4 = mybir.dt.float4_e2m1fn_x4
 MULT = mybir.AluOpType.mult
-ADD = mybir.AluOpType.add
+SUB = mybir.AluOpType.subtract
+MAX = mybir.AluOpType.max
+MIN = mybir.AluOpType.min
 COPY = mybir.ActivationFunctionType.Copy
 ABS = mybir.ActivationFunctionType.Abs
 
@@ -41,18 +43,24 @@ def tile_list_graft_union_features_kernel(
             return tile
 
         def zeroed_plane(shape, name):
-            tile = keep.tile(shape, U8, name=name, align_bytes=64)
+            tile = keep.tile(shape, U8, name=name, tag=name, align_bytes=64)
             nc.vector.memset(tile[:].bitcast(I32), 0)
             return tile
 
-        def load_table_scales(src, name):
-            passes = src.shape[0]
-            tile = zeroed_plane([P, T], name)
+        def load_table_scales(src, tag):
+            tile = keep.tile([P, src.shape[2]], U8, name="table_scales", tag=tag, align_bytes=64)
             for q in range(QUADS):
-                nc.scalar.dma_start(
-                    tile[32 * q : 32 * q + 4 * passes, :].bitcast(I32), src[:, 4 * q : 4 * q + 4, :].bitcast(I32)
+                quad_rows = src[0, 4 * q : 4 * q + 4, :].bitcast(I32)
+                nc.sync.dma_start(
+                    tile[32 * q : 32 * (q + 1), :].bitcast(I32), quad_rows.unsqueeze(0).to_broadcast([8, 4, src.shape[2] // 4])
                 )
             return tile
+
+        def load_scale_rows(tile, src):
+            for q in range(QUADS):
+                nc.sync.dma_start(
+                    tile[32 * q : 32 * q + 4 * src.shape[0], :].bitcast(I32), src[:, 4 * q : 4 * q + 4, :].bitcast(I32)
+                )
 
         def load_weight_scales(src, name, queue):
             passes = src.shape[0]
@@ -65,7 +73,7 @@ def tile_list_graft_union_features_kernel(
             return tile
 
         def load_table_words(src, tag):
-            tile = keep.tile([P, T], U32, name=tag, tag=tag, align_bytes=64)
+            tile = keep.tile([P, T], U32, name="words", tag=tag, align_bytes=64)
             nc.sync.dma_start(tile[:].bitcast(I32), src.rearrange("p t i -> p (t i)").bitcast(I32))
             return tile
 
@@ -74,37 +82,44 @@ def tile_list_graft_union_features_kernel(
             nc.vector.tensor_copy(tile[:], window[:].indirect(offsets[:]))
             return tile
 
+        def load_wa(raw, lo, hi):
+            nc.sync.dma_start(raw, wa[:, lo:hi].rearrange("(p t) c -> p t c", t=4))
+
+        t2s = keep.tile([P, T], U8, name="t2s", align_bytes=64)
+        nc.gpsimd.memset(t2s[:].bitcast(I32), 0)
         ident = keep.tile([P, P], F32, name="ident")
         make_identity(nc, ident[:])
-
+        w4s = load_weight_scales(w4_scales, "w4s", nc.gpsimd)
+        idx1 = load_list(offs, "idx1")
+        t1s = load_table_scales(tab_scales, "t1s")
+        wa_front = keep.tile([P, 2, 4, 256], F32, name="wa_front", tag="big1", align_bytes=64)
+        load_wa(wa_front[:, 0], 0, 256)
+        t1w = load_table_words(tab_words[0], "big0")
+        load_wa(wa_front[:, 1], 256, 512)
         idx3 = load_list(offs3, "idx3")
         t3s = load_table_scales(tab3_scales, "t3s")
-        t3w = load_table_words(tab3_words[0], "big0")
-        idx1 = load_list(offs, "idx1")
-        t1w = load_table_words(tab_words[0], "big1")
-        w8s = load_weight_scales(w8_scales, "w8s", nc.scalar)
+        t3w = load_table_words(tab3_words[0], "big2")
         w8w = keep.tile([P, H], U32, name="w8w", align_bytes=64)
         nc.sync.dma_start(w8w[:].bitcast(I32), w8_words[0].rearrange("p c i -> p (c i)").bitcast(I32))
-        t1s = load_table_scales(tab_scales, "t1s")
+        gain_rows = keep.tile([P, P], F32, name="gain_rows")
+        nc.sync.dma_start(
+            gain_rows[:], gz.rearrange("(s p) -> s p", p=P).unsqueeze(0).to_broadcast([P // 8, 8, P])
+        )
+        w8s = load_table_scales(w8_scales, "w8s")
+        wa_rest = keep.tile([P, 4, 512], F32, name="wa_rest", tag="big3", align_bytes=64)
+        load_wa(wa_rest[:], 512, H)
         idx2 = load_list(offs2, "idx2")
-        wa_raw = []
-        for h in range(2):
-            raw = ring.tile([P, 4, BANK], F32, name="raw", tag="raw", align_bytes=64)
-            nc.sync.dma_start(raw[:], wa[:, h * BANK : (h + 1) * BANK].rearrange("(p t) c -> p t c", t=4))
-            wa_raw.append(raw)
-        t2s = load_table_scales(tab2_scales, "t2s")
-        t2w = [load_table_words(tab2_words[a], "big%d" % (2 + a)) for a in range(2)]
-        p3 = load_list(pos3, "p3")
+        load_scale_rows(t2s, tab2_scales)
+        t2w = [load_table_words(tab2_words[a], "big%d" % (4 + a)) for a in range(2)]
         w4w = keep.tile([P, 2, 2 * H], U8, name="w4w", align_bytes=64)
         nc.sync.dma_start(w4w[:].bitcast(I32), w4_words.rearrange("a p b -> p a b").bitcast(I32))
-        w4s = load_weight_scales(w4_scales, "w4s", nc.sync)
         p1 = load_list(pos1, "p1")
+        p3 = load_list(pos3, "p3")
         p2 = load_list(pos2, "p2")
-        gain = keep.tile([P, H], F32, name="gain")
-        nc.sync.dma_start(gain[:], gz.partition_broadcast(P))
+        v2s_hi = zeroed_plane([P, S], "v2s_hi")
 
-        def first_stage(s, passes, tag, bufs, sign):
-            window = ring.tile([P, S], F32, name=tag, tag=tag, bufs=bufs)
+        def first_stage(passes, tag, scale, bufs):
+            window = ring.tile([P, S], F32, name=tag, tag=tag, bufs=bufs, align_bytes=64)
             for h in range(S // BANK):
                 cols = slice(h * BANK, (h + 1) * BANK)
                 acc = psum.tile([P, BANK], F32, name="mm", tag="mm", bufs=4)
@@ -113,141 +128,158 @@ def tile_list_graft_union_features_kernel(
                         out=acc[:], lhsT=w, lhsT_scale=ws, rhs=v[:, cols].bitcast(FP8X4), rhs_scale=vs[:, cols],
                         start=(i == 0), stop=(i == len(passes) - 1),
                     )
-                nc.scalar.activation(window[:, cols], acc[:], COPY, scale=sign)
+                nc.scalar.activation(window[:, cols], acc[:], COPY, scale=scale)
             return window
 
         def quantise(grouped, codes, scales):
             nc.vector.quantize_mx(out=codes.bitcast(FP8X4), scales=scales, in_=grouped)
 
-        v3s = gather_bytes(t3s, idx3, U8, "v3s")
-        v3w = gather_bytes(t3w, idx3, U32, "v3w")
-        rows = [slice(s * P, (s + 1) * P) for s in range(H // P)]
-        d_win = [
-            first_stage(s, [(w8w[:, rows[s]].bitcast(FP8X4), w8s[:, 0, rows[s]], v3w, v3s)], "d_win", 8, -1.0)
-            for s in range(H // P)
-        ]
-        v1w = gather_bytes(t1w, idx1, U32, "v1w")
-        v1s = gather_bytes(t1s, idx1, U8, "v1s")
-        v2s = gather_bytes(t2s, idx2, U8, "v2s")
-        v2s_hi = zeroed_plane([P, S], "v2s_hi")
-        nc.sync.dma_start(v2s_hi[0 : P - 4, :].bitcast(I32), v2s[4:P, :].bitcast(I32))
-        wa_c, wa_s = [], []
-        for h in range(2):
-            grouped = ring.tile([P, 4 * BANK], BF16, name="grouped", tag="grouped", bufs=3, align_bytes=64)
-            nc.gpsimd.tensor_scalar(
-                grouped[:].rearrange("p (c t) -> p c t", t=4), wa_raw[h][:].rearrange("p t c -> p c t"),
-                1.0, 0.0, MULT, ADD,
+        wa_q = {}
+
+        def quantise_wa(raw, lo):
+            width = raw.shape[2]
+            grouped = ring.tile([P, 4 * width], BF16, name="wa_g", tag="grouped", align_bytes=64)
+            nc.scalar.copy(
+                grouped[:].rearrange("p (c i t) -> p c t i", i=4, t=4), raw.rearrange("p t (c i) -> p c t i", i=4)
             )
-            codes = keep.tile([P, BANK], U32, name="wa_c%d" % h, align_bytes=64)
-            scales = keep.tile([P, BANK], U8, name="wa_s%d" % h, align_bytes=64)
+            codes = keep.tile([P, width], U32, name="wa_c%d" % lo, align_bytes=64)
+            scales = keep.tile([P, width], U8, name="wa_s%d" % lo, align_bytes=64)
             quantise(grouped[:], codes[:], scales[:])
-            wa_c.append(codes)
-            wa_s.append(scales)
-        v2w = [gather_bytes(t2w[a], idx2, U32, "v2w%d" % a) for a in range(2)]
-        v2_planes = [v2s, v2s_hi]
+            for i in range(width // P):
+                wa_q[lo // P + i] = (codes[:, rows[i]].bitcast(FP8X4), scales[:, rows[i]])
 
-        def pick(window, positions, lo, hi, tag, bufs):
-            tile = ring.tile([P, hi - lo], F32, name=tag, tag=tag, bufs=bufs)
-            nc.vector.tensor_copy(tile[:], window[:].indirect(positions[:, lo // 16 : hi // 16]))
-            return tile
+        rows = [slice(s * P, (s + 1) * P) for s in range(H // P)]
+        a_win, b_win, d_win = {}, {}, {}
 
-        a_win, b_win = {}, {}
+        def scions(s):
+            a_win[s] = first_stage([wa_q[s] + (v1w, v1s)], "a_win", 1.0, 6)
 
-        def scions_and_rootstocks(s):
-            local = slice((s % 4) * P, (s % 4 + 1) * P)
-            a_win[s] = first_stage(
-                s, [(wa_c[s // 4][:, local].bitcast(FP8X4), wa_s[s // 4][:, local], v1w, v1s)], "a_win", 5, 1.0
-            )
+        def rootstocks(s):
             b_win[s] = first_stage(
-                s,
                 [
                     (w4w[:, a, 2 * s * P : 2 * (s + 1) * P].bitcast(FP4X4), w4s[:, a, rows[s]], v2w[a], v2_planes[a])
                     for a in range(2)
                 ],
-                "b_win", 5, -1.0,
+                "b_win", 1.0, 5,
             )
 
-        def join(s, lo, hi, d1, z_t):
+        def soils(s):
+            d_win[s] = first_stage(
+                [(w8w[:, rows[s]].bitcast(FP8X4), w8s[:, rows[s]], v3w, v3s)], "d_win", gain[:, s : s + 1], 6
+            )
+
+        def work(width, tag, bufs=3):
+            return ring.tile([P, width], F32, name=tag, tag=tag, bufs=bufs)
+
+        def pick(window, positions, lo, hi, tag):
+            tile = work(hi - lo, tag, 3)
+            nc.vector.tensor_copy(tile[:], window[:].indirect(positions[:, lo // 16 : hi // 16]))
+            return tile
+
+        def join(s, lo, hi, z_t, on_vector):
             width = hi - lo
             blocks = width // P
-            a1 = pick(a_win[s], p1, lo, hi, "a1", 3)
-            b1 = pick(b_win[s], p2, lo, hi, "b1", 3)
-            diff = ring.tile([P, width], F32, name="diff", tag="diff", bufs=2)
-            nc.gpsimd.tensor_tensor(diff[:], a1[:], b1[:], ADD)
-            prod = ring.tile([P, width], F32, name="prod", tag="prod", bufs=2)
-            nc.gpsimd.tensor_tensor(prod[:], a1[:], b1[:], MULT)
-            dist = ring.tile([P, width], F32, name="dist", tag="dist", bufs=2)
-            nc.scalar.activation(dist[:], diff[:], ABS)
+            g_col, minus_g_col = gain[:, s : s + 1], minus_gain[:, s : s + 1]
+            a1 = pick(a_win[s], p1, lo, hi, "a1")
+            b1 = pick(b_win[s], p2, lo, hi, "b1")
+            diff = work(width, "diff")
+            nc.vector.tensor_tensor(diff[:], a1[:], b1[:], SUB)
+            prod = work(width, "prod")
+            nc.vector.scalar_tensor_tensor(prod[:], a1[:], g_col, b1[:], MULT, MULT)
+            below, above = work(width, "below"), work(width, "above")
+            if on_vector:
+                nc.vector.tensor_scalar(below[:], diff[:], 0.0, g_col, MIN, MULT)
+                nc.vector.tensor_scalar(above[:], diff[:], 0.0, minus_g_col, MAX, MULT)
+                d1 = a1
+                nc.vector.tensor_copy(d1[:], d_win[s][:].indirect(p3[:, lo // 16 : hi // 16]))
+                terms = (below, above, prod, d1)
+            else:
+                d1 = pick(d_win[s], p3, lo, hi, "d1")
+                nc.scalar.activation(below[:], diff[:], ABS)
+                nc.scalar.activation(above[:], below[:], COPY, scale=minus_g_col)
+                terms = (above, prod, d1)
             total = psum.tile([P, blocks, P], F32, name="total", tag="total")
-            terms = (d1, prod, dist)
             for i, term in enumerate(terms):
                 for b in range(blocks):
                     nc.tensor.matmul(
-                        total[:, b, :], term[:, b * P : (b + 1) * P], ident[:], is_transpose=True,
+                        total[:, b, :], term[:, rows[b]], ident[:], is_transpose=True,
                         start=(i == 0 and b == 0), stop=(i == len(terms) - 1 and b == blocks - 1),
                     )
-            nc.vector.scalar_tensor_tensor(
-                z_t[:, :, (s % 4) * P : (s % 4 + 1) * P], total[:], -1.0,
-                gain[:, rows[s]].unsqueeze(1).to_broadcast([P, blocks, P]), MULT, MULT,
-            )
+            nc.scalar.copy(z_t[:, :, rows[s % 4]], total[:])
 
         z_c, z_s = {}, {}
 
-        def turn_and_quantise(g, half, z_t, first_block):
-            words = z_t[:].rearrange("p b r -> p (b r)").bitcast(F32)
-            turned = psum.tile([P, 2, 2, P], F32, name="turned", tag="turned")
-            for b in range(2):
-                base = (first_block + b) * 256
-                for u in range(2):
-                    nc.tensor.transpose(turned[:, b, u, :], words[:, base + u : base + 256 : 2], ident[:])
-            grouped = ring.tile([P, 4 * 256], BF16, name="grouped", tag="grouped", bufs=3, align_bytes=64)
-            nc.scalar.copy(
-                grouped[:].bitcast(F32).rearrange("p (b j u) -> p b j u", b=2, u=2),
-                turned[:].rearrange("p b u j -> p b j u"),
+        def turn_and_quantise(g, block, z_t, local, engine):
+            words = z_t[:, local, :].bitcast(F32)
+            turned = psum.tile([P, 2, P], F32, name="turned", tag="turned")
+            for u in range(2):
+                nc.tensor.transpose(turned[:, u, :], words[:, u:256:2], ident[:])
+            grouped = ring.tile([P, 4 * P], BF16, name="z_g", tag="small_grouped", bufs=3, align_bytes=64)
+            engine(
+                grouped[:].bitcast(F32).rearrange("p (j u) -> p j u", u=2), turned[:].rearrange("p u j -> p j u")
             )
-            z_c[g, half] = keep.tile([P, 256], U32, name="z_c%d%d" % (g, half), align_bytes=64)
-            z_s[g, half] = keep.tile([P, 256], U8, name="z_s%d%d" % (g, half), align_bytes=64)
-            quantise(grouped[:], z_c[g, half][:], z_s[g, half][:])
-
-        d1_first = [pick(d_win[s], p3, 0, NU, "d1", 4) for s in range(4)]
-        d1_a = [pick(d_win[s], p3, 0, 256, "d1h", 4) for s in range(4, 8)]
-
-        scions_and_rootstocks(0)
-        scions_and_rootstocks(1)
-        z_t0 = keep.tile([P, 4, BANK], BF16, name="z_t0", tag="big2", align_bytes=64)
-        for s in range(4):
-            scions_and_rootstocks(s + 2)
-            join(s, 0, NU, d1_first[s], z_t0)
+            z_c[g, block] = keep.tile([P, P], U32, name="z_c%d%d" % (g, block), align_bytes=64)
+            z_s[g, block] = keep.tile([P, P], U8, name="z_s%d%d" % (g, block), align_bytes=64)
+            quantise(grouped[:], z_c[g, block][:], z_s[g, block][:])
 
         wy_c, wy_s = [], []
-        for g in range(2):
-            raw = keep.tile([P, 4, N], F32, name="wy_raw", tag="big%d" % g, align_bytes=64)
+
+        def quantise_wy(g):
+            raw = keep.tile([P, 4, N], F32, name="wy_raw", tag="big%d" % (4 + g), align_bytes=64)
             nc.sync.dma_start(raw[:], wy[g * 512 : (g + 1) * 512, :].rearrange("(p j) n -> p j n", j=4))
-            grouped = ring.tile([P, 4 * N], BF16, name="grouped", tag="grouped", bufs=3, align_bytes=64)
+            grouped = ring.tile([P, 4 * N], BF16, name="wy_g", tag="b_win", bufs=5, align_bytes=64)
             nc.scalar.copy(
                 grouped[:].rearrange("p (t m j) -> p m j t", t=4, j=4),
                 raw[:].rearrange("p j (m t) -> p m j t", t=4),
             )
-            codes = keep.tile([P, N], U32, name="wy_c%d" % g, align_bytes=64)
-            scales = keep.tile([P, N], U8, name="wy_s%d" % g, align_bytes=64)
-            quantise(grouped[:], codes[:], scales[:])
-            wy_c.append(codes)
-            wy_s.append(scales)
+            wy_c.append(keep.tile([P, N], U32, name="wy_c%d" % g, align_bytes=64))
+            wy_s.append(keep.tile([P, N], U8, name="wy_s%d" % g, align_bytes=64))
+            quantise(grouped[:], wy_c[g][:], wy_s[g][:])
 
-        scions_and_rootstocks(6)
-        scions_and_rootstocks(7)
-        for half in range(2):
-            turn_and_quantise(0, half, z_t0, 2 * half)
+        v1s = gather_bytes(t1s, idx1, U8, "v1s")
+        quantise_wa(wa_front[:, 0], 0)
+        v1w = gather_bytes(t1w, idx1, U32, "v1w")
+        v3s = gather_bytes(t3s, idx3, U8, "v3s")
+        quantise_wa(wa_front[:, 1], 256)
+        v3w = gather_bytes(t3w, idx3, U32, "v3w")
+        v2s = gather_bytes(t2s, idx2, U8, "v2s")
+        nc.sync.dma_start(v2s_hi[0 : P - 4, :].bitcast(I32), v2s[4:P, :].bitcast(I32))
+        v2w = [gather_bytes(t2w[a], idx2, U32, "v2w%d" % a) for a in range(2)]
+        v2_planes = [v2s, v2s_hi]
+        for s in range(4):
+            scions(s)
+        gain_turned = psum.tile([P, P], F32, name="gain_turned", tag="turned")
+        nc.tensor.transpose(gain_turned[:], gain_rows[:], ident[:])
+        gain = keep.tile([P, H // P], F32, name="gain")
+        minus_gain = keep.tile([P, H // P], F32, name="minus_gain")
+        nc.scalar.copy(gain[:], gain_turned[:, 0 : H // P])
+        nc.scalar.activation(minus_gain[:], gain_turned[:, 0 : H // P], COPY, scale=-1.0)
+        for s in range(5):
+            soils(s)
+        quantise_wa(wa_rest[:], 512)
+        for s in range(5):
+            rootstocks(s)
+        scions(4)
+        quantise_wy(0)
+        z_t0 = keep.tile([P, 4, BANK], BF16, name="z_t0", tag="big0", align_bytes=64)
+        for s in range(4):
+            join(s, 0, NU, z_t0, False)
+            if s == 0:
+                quantise_wy(1)
+            else:
+                for stage in (scions, rootstocks, soils):
+                    stage(s + 4)
+        for block in range(4):
+            turn_and_quantise(0, block, z_t0, block, nc.scalar.copy)
 
         y_acc = [psum.tile([P, 4, P], F32, name="mm", tag="mm", bufs=4) for b in range(4)]
 
         def last_stage(g, block):
-            cols = slice((block % 2) * P, (block % 2 + 1) * P)
             for t in range(4):
                 nc.tensor.matmul_mx(
                     out=y_acc[block][:, t, :],
                     lhsT=wy_c[g][:, t * P : (t + 1) * P].bitcast(FP8X4), lhsT_scale=wy_s[g][:, t * P : (t + 1) * P],
-                    rhs=z_c[g, block // 2][:, cols].bitcast(FP8X4), rhs_scale=z_s[g, block // 2][:, cols],
+                    rhs=z_c[g, block][:].bitcast(FP8X4), rhs_scale=z_s[g, block][:],
                     start=(g == 0 and t == 0), stop=(g == 1 and t == 3),
                 )
 
@@ -256,28 +288,30 @@ def tile_list_graft_union_features_kernel(
         y_rows = out_0.rearrange("(p t) j -> p t j", t=4)
         code_rows = out_1[0].rearrange("p m t -> p (m t)").bitcast(I32)
 
-        z_t1 = ring.tile([P, 2, BANK], BF16, name="z_t1", tag="z_t1", align_bytes=64)
-        for s in range(4, 8):
-            join(s, 0, 256, d1_a[s - 4], z_t1)
-        for block in range(4):
-            last_stage(0, block)
         for half in range(2):
-            if half == 1:
-                z_t1 = ring.tile([P, 2, BANK], BF16, name="z_t1", tag="z_t1", align_bytes=64)
-                for s in range(4, 8):
-                    join(s, 256, NU, pick(d_win[s], p3, 256, NU, "d1h", 4), z_t1)
-            turn_and_quantise(1, half, z_t1, 0)
-            y_sb = ring.tile([P, 4, 256], F32, name="raw", tag="raw", align_bytes=64)
+            z_t1 = ring.tile([P, 2, BANK], BF16, name="z_t1", tag="z_t1", align_bytes=64)
+            for s in range(4, 8):
+                join(s, half * 256, (half + 1) * 256, z_t1, half == 1)
+            if half == 0:
+                for block in range(4):
+                    last_stage(0, block)
+            y_sb = keep.tile([P, 4, 256], F32, name="y_sb", tag="big%d" % (1 + half), align_bytes=64)
+            for b in range(2):
+                engine = nc.vector.tensor_copy if half == 1 and b == 1 else nc.scalar.copy
+                turn_and_quantise(1, 2 * half + b, z_t1, b, engine)
+            for b in range(2):
+                last_stage(1, 2 * half + b)
+                engine = nc.vector.tensor_copy if half == 1 and b == 1 else nc.scalar.copy
+                engine(y_sb[:, :, rows[b]], y_acc[2 * half + b][:])
             for b in range(2):
                 block = 2 * half + b
-                last_stage(1, block)
-                grouped = ring.tile([P, 4 * P], BF16, name="grouped", tag="grouped", bufs=3, align_bytes=64)
-                nc.vector.tensor_copy(
-                    grouped[:].rearrange("p (j t) -> p j t", t=4), y_acc[block][:].rearrange("p t j -> p j t")
+                grouped = ring.tile([P, 4 * P], BF16, name="y_g", tag="small_grouped", bufs=3, align_bytes=64)
+                engine = nc.vector.tensor_copy if half == 1 and b == 1 else nc.scalar.copy
+                engine(
+                    grouped[:].rearrange("p (c i t) -> p c t i", i=4, t=4),
+                    y_sb[:, :, rows[b]].rearrange("p t (c i) -> p c t i", i=4),
                 )
-                nc.scalar.copy(y_sb[:, :, b * P : (b + 1) * P], y_acc[block][:])
-                cols = slice(block * P, (block + 1) * P)
-                quantise(grouped[:], y_codes[:, cols], y_scales[:, cols])
+                quantise(grouped[:], y_codes[:, rows[block]], y_scales[:, rows[block]])
             cols = slice(half * 256, (half + 1) * 256)
             nc.sync.dma_start(y_rows[:, :, cols], y_sb[:])
             nc.sync.dma_start(code_rows[:, cols], y_codes[:, cols].bitcast(I32))

@@ -24,6 +24,9 @@ ABS = mybir.ActivationFunctionType.Abs
 P = 128
 BANK = 512
 QUADS = 4
+HOLD = 7
+VFROM = 7
+NP = 2
 
 
 def tile_list_graft_union_features_kernel(
@@ -58,7 +61,7 @@ def tile_list_graft_union_features_kernel(
 
         def load_scale_rows(tile, src):
             for q in range(QUADS):
-                nc.sync.dma_start(
+                nc.gpsimd.dma_start(
                     tile[32 * q : 32 * q + 4 * src.shape[0], :].bitcast(I32), src[:, 4 * q : 4 * q + 4, :].bitcast(I32)
                 )
 
@@ -87,6 +90,7 @@ def tile_list_graft_union_features_kernel(
 
         t2s = keep.tile([P, T], U8, name="t2s", align_bytes=64)
         nc.gpsimd.memset(t2s[:].bitcast(I32), 0)
+        load_scale_rows(t2s, tab2_scales)
         ident = keep.tile([P, P], F32, name="ident")
         make_identity(nc, ident[:])
         w4s = load_weight_scales(w4_scales, "w4s", nc.gpsimd)
@@ -101,16 +105,16 @@ def tile_list_graft_union_features_kernel(
         t3w = load_table_words(tab3_words[0], "big2")
         w8w = keep.tile([P, H], U32, name="w8w", align_bytes=64)
         nc.sync.dma_start(w8w[:].bitcast(I32), w8_words[0].rearrange("p c i -> p (c i)").bitcast(I32))
+        idx2 = load_list(offs2, "idx2")
         gain_rows = keep.tile([P, P], F32, name="gain_rows")
         nc.sync.dma_start(
             gain_rows[:], gz.rearrange("(s p) -> s p", p=P).unsqueeze(0).to_broadcast([P // 8, 8, P])
         )
         w8s = load_table_scales(w8_scales, "w8s")
+        t2w = [load_table_words(tab2_words[0], "big4")]
         wa_rest = keep.tile([P, 4, 512], F32, name="wa_rest", tag="big3", align_bytes=64)
         load_wa(wa_rest[:], 512, H)
-        idx2 = load_list(offs2, "idx2")
-        load_scale_rows(t2s, tab2_scales)
-        t2w = [load_table_words(tab2_words[a], "big%d" % (4 + a)) for a in range(2)]
+        t2w.append(load_table_words(tab2_words[1], "big5"))
         w4w = keep.tile([P, 2, 2 * H], U8, name="w4w", align_bytes=64)
         nc.sync.dma_start(w4w[:].bitcast(I32), w4_words.rearrange("a p b -> p a b").bitcast(I32))
         p1 = load_list(pos1, "p1")
@@ -172,7 +176,7 @@ def tile_list_graft_union_features_kernel(
             return ring.tile([P, width], F32, name=tag, tag=tag, bufs=bufs)
 
         def pick(window, positions, lo, hi, tag):
-            tile = work(hi - lo, tag, 3)
+            tile = work(hi - lo, tag, NP)
             nc.vector.tensor_copy(tile[:], window[:].indirect(positions[:, lo // 16 : hi // 16]))
             return tile
 
@@ -180,7 +184,11 @@ def tile_list_graft_union_features_kernel(
             width = hi - lo
             blocks = width // P
             g_col, minus_g_col = gain[:, s : s + 1], minus_gain[:, s : s + 1]
-            a1 = pick(a_win[s], p1, lo, hi, "a1")
+            if on_vector and s == HOLD:
+                a1 = ring.tile([P, width], F32, name="a1_held", tag="z_g", align_bytes=64)
+                nc.vector.tensor_copy(a1[:], a_win[s][:].indirect(p1[:, lo // 16 : hi // 16]))
+            else:
+                a1 = pick(a_win[s], p1, lo, hi, "a1")
             b1 = pick(b_win[s], p2, lo, hi, "b1")
             diff = work(width, "diff")
             nc.vector.tensor_tensor(diff[:], a1[:], b1[:], SUB)
@@ -214,7 +222,7 @@ def tile_list_graft_union_features_kernel(
             turned = psum.tile([P, 2, P], F32, name="turned", tag="turned")
             for u in range(2):
                 nc.tensor.transpose(turned[:, u, :], words[:, u:256:2], ident[:])
-            grouped = ring.tile([P, 4 * P], BF16, name="z_g", tag="small_grouped", bufs=3, align_bytes=64)
+            grouped = ring.tile([P, 4 * P], BF16, name="z_g", tag="z_g", align_bytes=64)
             engine(
                 grouped[:].bitcast(F32).rearrange("p (j u) -> p j u", u=2), turned[:].rearrange("p u j -> p j u")
             )
@@ -225,7 +233,7 @@ def tile_list_graft_union_features_kernel(
         wy_c, wy_s = [], []
 
         def quantise_wy(g):
-            raw = keep.tile([P, 4, N], F32, name="wy_raw", tag="big%d" % (4 + g), align_bytes=64)
+            raw = keep.tile([P, 4, N], F32, name="wy_raw", tag="big%d" % (5 - 2 * g), align_bytes=64)
             nc.sync.dma_start(raw[:], wy[g * 512 : (g + 1) * 512, :].rearrange("(p j) n -> p j n", j=4))
             grouped = ring.tile([P, 4 * N], BF16, name="wy_g", tag="b_win", bufs=5, align_bytes=64)
             nc.scalar.copy(
@@ -291,7 +299,7 @@ def tile_list_graft_union_features_kernel(
         for half in range(2):
             z_t1 = ring.tile([P, 2, BANK], BF16, name="z_t1", tag="z_t1", align_bytes=64)
             for s in range(4, 8):
-                join(s, half * 256, (half + 1) * 256, z_t1, half == 1)
+                join(s, half * 256, (half + 1) * 256, z_t1, half == 1 and s >= VFROM)
             if half == 0:
                 for block in range(4):
                     last_stage(0, block)
@@ -305,7 +313,7 @@ def tile_list_graft_union_features_kernel(
                 engine(y_sb[:, :, rows[b]], y_acc[2 * half + b][:])
             for b in range(2):
                 block = 2 * half + b
-                grouped = ring.tile([P, 4 * P], BF16, name="y_g", tag="small_grouped", bufs=3, align_bytes=64)
+                grouped = ring.tile([P, 4 * P], BF16, name="y_g", tag="y_g", align_bytes=64)
                 engine = nc.vector.tensor_copy if half == 1 and b == 1 else nc.scalar.copy
                 engine(
                     grouped[:].rearrange("p (c i t) -> p c t i", i=4, t=4),

from contextlib import ExitStack

import concourse.mybir as mybir
from concourse.masks import make_identity

K, K2, T, S, NU, H, N = 512, 1024, 2048, 1024, 512, 1024, 512
FLOPS = 2 * (K + K2 + K) * H * S + 2 * H * N * NU

F32 = mybir.dt.float32
BF16 = mybir.dt.bfloat16
I32 = mybir.dt.int32
U32 = mybir.dt.uint32
U16 = mybir.dt.uint16
U8 = mybir.dt.uint8
FP8X4 = mybir.dt.float8_e4m3fn_x4
FP4X4 = mybir.dt.float4_e2m1fn_x4
MULT = mybir.AluOpType.mult
SUB = mybir.AluOpType.subtract
MAX = mybir.AluOpType.max
MIN = mybir.AluOpType.min
COPY = mybir.ActivationFunctionType.Copy
ABS = mybir.ActivationFunctionType.Abs

P = 128
BANK = 512
QUADS = 4
HOLD = 7
VFROM = 7
NP = 2


def tile_list_graft_union_features_kernel(
    tc, tab_words, tab_scales, tab2_words, tab2_scales, tab3_words, tab3_scales, offs, offs2, offs3,
    pos1, pos2, pos3, wa, w4_words, w4_scales, w8_words, w8_scales, gz, wy, out_0, out_1, out_2,
):
    nc = tc.nc
    with ExitStack() as ctx:
        lists = ctx.enter_context(tc.tile_pool(name="lists", bufs=1))
        keep = ctx.enter_context(tc.tile_pool(name="keep", bufs=1))
        ring = ctx.enter_context(tc.tile_pool(name="ring", bufs=2))
        psum = ctx.enter_context(tc.psum_pool(name="psum", bufs=2))

        def load_list(src, name):
            tile = lists.tile(list(src.shape), U16, name=name)
            nc.sync.dma_start(tile[:], src)
            return tile

        def zeroed_plane(shape, name):
            tile = keep.tile(shape, U8, name=name, tag=name, align_bytes=64)
            nc.vector.memset(tile[:].bitcast(I32), 0)
            return tile

        def load_table_scales(src, tag):
            tile = keep.tile([P, src.shape[2]], U8, name="table_scales", tag=tag, align_bytes=64)
            for q in range(QUADS):
                quad_rows = src[0, 4 * q : 4 * q + 4, :].bitcast(I32)
                nc.sync.dma_start(
                    tile[32 * q : 32 * (q + 1), :].bitcast(I32), quad_rows.unsqueeze(0).to_broadcast([8, 4, src.shape[2] // 4])
                )
            return tile

        def load_scale_rows(tile, src):
            for q in range(QUADS):
                nc.gpsimd.dma_start(
                    tile[32 * q : 32 * q + 4 * src.shape[0], :].bitcast(I32), src[:, 4 * q : 4 * q + 4, :].bitcast(I32)
                )

        def load_weight_scales(src, name, queue):
            passes = src.shape[0]
            tile = zeroed_plane([P, passes, H], name)
            for q in range(QUADS):
                queue.dma_start(
                    tile[32 * q : 32 * q + 4, :, :].bitcast(I32),
                    src[:, 4 * q : 4 * q + 4, :].rearrange("a r n -> r a n").bitcast(I32),
                )
            return tile

        def load_table_words(src, tag):
            tile = keep.tile([P, T], U32, name="words", tag=tag, align_bytes=64)
            nc.sync.dma_start(tile[:].bitcast(I32), src.rearrange("p t i -> p (t i)").bitcast(I32))
            return tile

        def gather_bytes(window, offsets, dtype, name):
            tile = keep.tile([P, S], dtype, name=name, align_bytes=64)
            nc.vector.tensor_copy(tile[:], window[:].indirect(offsets[:]))
            return tile

        def load_wa(raw, lo, hi):
            nc.sync.dma_start(raw, wa[:, lo:hi].rearrange("(p t) c -> p t c", t=4))

        t2s = keep.tile([P, T], U8, name="t2s", align_bytes=64)
        nc.gpsimd.memset(t2s[:].bitcast(I32), 0)
        load_scale_rows(t2s, tab2_scales)
        ident = keep.tile([P, P], F32, name="ident")
        make_identity(nc, ident[:])
        w4s = load_weight_scales(w4_scales, "w4s", nc.gpsimd)
        idx1 = load_list(offs, "idx1")
        t1s = load_table_scales(tab_scales, "t1s")
        wa_front = keep.tile([P, 2, 4, 256], F32, name="wa_front", tag="big1", align_bytes=64)
        load_wa(wa_front[:, 0], 0, 256)
        t1w = load_table_words(tab_words[0], "big0")
        load_wa(wa_front[:, 1], 256, 512)
        idx3 = load_list(offs3, "idx3")
        t3s = load_table_scales(tab3_scales, "t3s")
        t3w = load_table_words(tab3_words[0], "big2")
        w8w = keep.tile([P, H], U32, name="w8w", align_bytes=64)
        nc.sync.dma_start(w8w[:].bitcast(I32), w8_words[0].rearrange("p c i -> p (c i)").bitcast(I32))
        idx2 = load_list(offs2, "idx2")
        gain_rows = keep.tile([P, P], F32, name="gain_rows")
        nc.sync.dma_start(
            gain_rows[:], gz.rearrange("(s p) -> s p", p=P).unsqueeze(0).to_broadcast([P // 8, 8, P])
        )
        w8s = load_table_scales(w8_scales, "w8s")
        t2w = [load_table_words(tab2_words[0], "big4")]
        wa_rest = keep.tile([P, 4, 512], F32, name="wa_rest", tag="big3", align_bytes=64)
        load_wa(wa_rest[:], 512, H)
        t2w.append(load_table_words(tab2_words[1], "big5"))
        w4w = keep.tile([P, 2, 2 * H], U8, name="w4w", align_bytes=64)
        nc.sync.dma_start(w4w[:].bitcast(I32), w4_words.rearrange("a p b -> p a b").bitcast(I32))
        p1 = load_list(pos1, "p1")
        p3 = load_list(pos3, "p3")
        p2 = load_list(pos2, "p2")
        v2s_hi = zeroed_plane([P, S], "v2s_hi")

        def first_stage(passes, tag, scale, bufs):
            window = ring.tile([P, S], F32, name=tag, tag=tag, bufs=bufs, align_bytes=64)
            for h in range(S // BANK):
                cols = slice(h * BANK, (h + 1) * BANK)
                acc = psum.tile([P, BANK], F32, name="mm", tag="mm", bufs=4)
                for i, (w, ws, v, vs) in enumerate(passes):
                    nc.tensor.matmul_mx(
                        out=acc[:], lhsT=w, lhsT_scale=ws, rhs=v[:, cols].bitcast(FP8X4), rhs_scale=vs[:, cols],
                        start=(i == 0), stop=(i == len(passes) - 1),
                    )
                nc.scalar.activation(window[:, cols], acc[:], COPY, scale=scale)
            return window

        def quantise(grouped, codes, scales):
            nc.vector.quantize_mx(out=codes.bitcast(FP8X4), scales=scales, in_=grouped)

        wa_q = {}

        def quantise_wa(raw, lo):
            width = raw.shape[2]
            grouped = ring.tile([P, 4 * width], BF16, name="wa_g", tag="grouped", align_bytes=64)
            nc.scalar.copy(
                grouped[:].rearrange("p (c i t) -> p c t i", i=4, t=4), raw.rearrange("p t (c i) -> p c t i", i=4)
            )
            codes = keep.tile([P, width], U32, name="wa_c%d" % lo, align_bytes=64)
            scales = keep.tile([P, width], U8, name="wa_s%d" % lo, align_bytes=64)
            quantise(grouped[:], codes[:], scales[:])
            for i in range(width // P):
                wa_q[lo // P + i] = (codes[:, rows[i]].bitcast(FP8X4), scales[:, rows[i]])

        rows = [slice(s * P, (s + 1) * P) for s in range(H // P)]
        a_win, b_win, d_win = {}, {}, {}

        def scions(s):
            a_win[s] = first_stage([wa_q[s] + (v1w, v1s)], "a_win", 1.0, 6)

        def rootstocks(s):
            b_win[s] = first_stage(
                [
                    (w4w[:, a, 2 * s * P : 2 * (s + 1) * P].bitcast(FP4X4), w4s[:, a, rows[s]], v2w[a], v2_planes[a])
                    for a in range(2)
                ],
                "b_win", 1.0, 5,
            )

        def soils(s):
            d_win[s] = first_stage(
                [(w8w[:, rows[s]].bitcast(FP8X4), w8s[:, rows[s]], v3w, v3s)], "d_win", gain[:, s : s + 1], 6
            )

        def work(width, tag, bufs=3):
            return ring.tile([P, width], F32, name=tag, tag=tag, bufs=bufs)

        def pick(window, positions, lo, hi, tag):
            tile = work(hi - lo, tag, NP)
            nc.vector.tensor_copy(tile[:], window[:].indirect(positions[:, lo // 16 : hi // 16]))
            return tile

        def join(s, lo, hi, z_t, on_vector):
            width = hi - lo
            blocks = width // P
            g_col, minus_g_col = gain[:, s : s + 1], minus_gain[:, s : s + 1]
            if on_vector and s == HOLD:
                a1 = ring.tile([P, width], F32, name="a1_held", tag="z_g", align_bytes=64)
                nc.vector.tensor_copy(a1[:], a_win[s][:].indirect(p1[:, lo // 16 : hi // 16]))
            else:
                a1 = pick(a_win[s], p1, lo, hi, "a1")
            b1 = pick(b_win[s], p2, lo, hi, "b1")
            diff = work(width, "diff")
            nc.vector.tensor_tensor(diff[:], a1[:], b1[:], SUB)
            prod = work(width, "prod")
            nc.vector.scalar_tensor_tensor(prod[:], a1[:], g_col, b1[:], MULT, MULT)
            below, above = work(width, "below"), work(width, "above")
            if on_vector:
                nc.vector.tensor_scalar(below[:], diff[:], 0.0, g_col, MIN, MULT)
                nc.vector.tensor_scalar(above[:], diff[:], 0.0, minus_g_col, MAX, MULT)
                d1 = a1
                nc.vector.tensor_copy(d1[:], d_win[s][:].indirect(p3[:, lo // 16 : hi // 16]))
                terms = (below, above, prod, d1)
            else:
                d1 = pick(d_win[s], p3, lo, hi, "d1")
                nc.scalar.activation(below[:], diff[:], ABS)
                nc.scalar.activation(above[:], below[:], COPY, scale=minus_g_col)
                terms = (above, prod, d1)
            total = psum.tile([P, blocks, P], F32, name="total", tag="total")
            for i, term in enumerate(terms):
                for b in range(blocks):
                    nc.tensor.matmul(
                        total[:, b, :], term[:, rows[b]], ident[:], is_transpose=True,
                        start=(i == 0 and b == 0), stop=(i == len(terms) - 1 and b == blocks - 1),
                    )
            nc.scalar.copy(z_t[:, :, rows[s % 4]], total[:])

        z_c, z_s = {}, {}

        def turn_and_quantise(g, block, z_t, local, engine):
            words = z_t[:, local, :].bitcast(F32)
            turned = psum.tile([P, 2, P], F32, name="turned", tag="turned")
            for u in range(2):
                nc.tensor.transpose(turned[:, u, :], words[:, u:256:2], ident[:])
            grouped = ring.tile([P, 4 * P], BF16, name="z_g", tag="z_g", align_bytes=64)
            engine(
                grouped[:].bitcast(F32).rearrange("p (j u) -> p j u", u=2), turned[:].rearrange("p u j -> p j u")
            )
            z_c[g, block] = keep.tile([P, P], U32, name="z_c%d%d" % (g, block), align_bytes=64)
            z_s[g, block] = keep.tile([P, P], U8, name="z_s%d%d" % (g, block), align_bytes=64)
            quantise(grouped[:], z_c[g, block][:], z_s[g, block][:])

        wy_c, wy_s = [], []

        def quantise_wy(g):
            raw = keep.tile([P, 4, N], F32, name="wy_raw", tag="big%d" % (5 - 2 * g), align_bytes=64)
            nc.sync.dma_start(raw[:], wy[g * 512 : (g + 1) * 512, :].rearrange("(p j) n -> p j n", j=4))
            grouped = ring.tile([P, 4 * N], BF16, name="wy_g", tag="b_win", bufs=5, align_bytes=64)
            nc.scalar.copy(
                grouped[:].rearrange("p (t m j) -> p m j t", t=4, j=4),
                raw[:].rearrange("p j (m t) -> p m j t", t=4),
            )
            wy_c.append(keep.tile([P, N], U32, name="wy_c%d" % g, align_bytes=64))
            wy_s.append(keep.tile([P, N], U8, name="wy_s%d" % g, align_bytes=64))
            quantise(grouped[:], wy_c[g][:], wy_s[g][:])

        v1s = gather_bytes(t1s, idx1, U8, "v1s")
        quantise_wa(wa_front[:, 0], 0)
        v1w = gather_bytes(t1w, idx1, U32, "v1w")
        v3s = gather_bytes(t3s, idx3, U8, "v3s")
        quantise_wa(wa_front[:, 1], 256)
        v3w = gather_bytes(t3w, idx3, U32, "v3w")
        v2s = gather_bytes(t2s, idx2, U8, "v2s")
        nc.sync.dma_start(v2s_hi[0 : P - 4, :].bitcast(I32), v2s[4:P, :].bitcast(I32))
        v2w = [gather_bytes(t2w[a], idx2, U32, "v2w%d" % a) for a in range(2)]
        v2_planes = [v2s, v2s_hi]
        for s in range(4):
            scions(s)
        gain_turned = psum.tile([P, P], F32, name="gain_turned", tag="turned")
        nc.tensor.transpose(gain_turned[:], gain_rows[:], ident[:])
        gain = keep.tile([P, H // P], F32, name="gain")
        minus_gain = keep.tile([P, H // P], F32, name="minus_gain")
        nc.scalar.copy(gain[:], gain_turned[:, 0 : H // P])
        nc.scalar.activation(minus_gain[:], gain_turned[:, 0 : H // P], COPY, scale=-1.0)
        for s in range(5):
            soils(s)
        quantise_wa(wa_rest[:], 512)
        for s in range(5):
            rootstocks(s)
        scions(4)
        quantise_wy(0)
        z_t0 = keep.tile([P, 4, BANK], BF16, name="z_t0", tag="big0", align_bytes=64)
        for s in range(4):
            join(s, 0, NU, z_t0, False)
            if s == 0:
                quantise_wy(1)
            else:
                for stage in (scions, rootstocks, soils):
                    stage(s + 4)
        for block in range(4):
            turn_and_quantise(0, block, z_t0, block, nc.scalar.copy)

        y_acc = [psum.tile([P, 4, P], F32, name="mm", tag="mm", bufs=4) for b in range(4)]

        def last_stage(g, block):
            for t in range(4):
                nc.tensor.matmul_mx(
                    out=y_acc[block][:, t, :],
                    lhsT=wy_c[g][:, t * P : (t + 1) * P].bitcast(FP8X4), lhsT_scale=wy_s[g][:, t * P : (t + 1) * P],
                    rhs=z_c[g, block][:].bitcast(FP8X4), rhs_scale=z_s[g, block][:],
                    start=(g == 0 and t == 0), stop=(g == 1 and t == 3),
                )

        y_codes = keep.tile([P, NU], U32, name="y_codes", align_bytes=64)
        y_scales = keep.tile([P, NU], U8, name="y_scales", align_bytes=64)
        y_rows = out_0.rearrange("(p t) j -> p t j", t=4)
        code_rows = out_1[0].rearrange("p m t -> p (m t)").bitcast(I32)

        for half in range(2):
            z_t1 = ring.tile([P, 2, BANK], BF16, name="z_t1", tag="z_t1", align_bytes=64)
            for s in range(4, 8):
                join(s, half * 256, (half + 1) * 256, z_t1, half == 1 and s >= VFROM)
            if half == 0:
                for block in range(4):
                    last_stage(0, block)
            y_sb = keep.tile([P, 4, 256], F32, name="y_sb", tag="big%d" % (1 + half), align_bytes=64)
            for b in range(2):
                engine = nc.vector.tensor_copy if half == 1 and b == 1 else nc.scalar.copy
                turn_and_quantise(1, 2 * half + b, z_t1, b, engine)
            for b in range(2):
                last_stage(1, 2 * half + b)
                engine = nc.vector.tensor_copy if half == 1 and b == 1 else nc.scalar.copy
                engine(y_sb[:, :, rows[b]], y_acc[2 * half + b][:])
            for b in range(2):
                block = 2 * half + b
                grouped = ring.tile([P, 4 * P], BF16, name="y_g", tag="y_g", align_bytes=64)
                engine = nc.vector.tensor_copy if half == 1 and b == 1 else nc.scalar.copy
                engine(
                    grouped[:].rearrange("p (c i t) -> p c t i", i=4, t=4),
                    y_sb[:, :, rows[b]].rearrange("p t (c i) -> p c t i", i=4),
                )
                quantise(grouped[:], y_codes[:, rows[block]], y_scales[:, rows[block]])
            cols = slice(half * 256, (half + 1) * 256)
            nc.sync.dma_start(y_rows[:, :, cols], y_sb[:])
            nc.sync.dma_start(code_rows[:, cols], y_codes[:, cols].bitcast(I32))
        for q in range(QUADS):
            queue = nc.sync if q % 2 == 0 else nc.scalar
            queue.dma_start(
                out_2[0, 4 * q : 4 * q + 4, :].bitcast(I32), y_scales[32 * q : 32 * q + 4, :].bitcast(I32)
            )
